import numpy as np
CORES = [3,5,19,21,35,37,51,53,67,69]
N = 10
W, KW, DIL = 128, 3, 8
H = (KW // 2) * DIL
def setup_inputs(rng):
    return {"x": rng.standard_normal((N, 128, W), dtype=np.float32), "w": rng.standard_normal((N, 128, KW * 128), dtype=np.float32)}
def setup_inputs_big(rng):
    d = setup_inputs(rng)
    for k in ("x", "w"): d[k] = (d[k].astype(np.float32) * 1024.0).astype(d[k].dtype)
    return d
def setup_inputs_small(rng):
    d = setup_inputs(rng)
    for k in ("x", "w"): d[k] = (d[k].astype(np.float32) * (1 / 1024.0)).astype(d[k].dtype)
    return d
def setup_inputs_apart(rng):
    d = setup_inputs(rng)
    f = (10.0 ** rng.permutation(np.linspace(-1.5, 1.5, N))).astype(np.float32).reshape(N, 1, 1)
    for k in ("x", "w"): d[k] = (d[k].astype(np.float32) * f).astype(d[k].dtype)
    return d
def reference(x, w):
    X, W_ = x.astype(np.float64), w.astype(np.float64)
    g = np.concatenate(list(X), axis=1)
    p = np.concatenate([g[:, -H:], g, g[:, :H]], axis=1)
    y = np.zeros((N, 128, W))
    for r in range(N):
        for i in range(KW):
            y[r] += W_[r][:, 128 * i:128 * i + 128].T @ p[:, W * r + i * DIL:W * r + i * DIL + W]
    return {"y": y.astype(np.float32 if x.dtype != np.float64 else np.float64)}

@@ -1,0 +1,84 @@
+from concourse.bass import DstId, RemoteDMATransfer
+
+P = 128
+W = 128
+H = 8
+K_FAR = 4
+K_NEAR = 4
+
+SCRATCH = {
+    "xs": ("sbuf", [P, W], "float32"),
+    "ws": ("sbuf", [P, 3 * P], "float32"),
+    "hl": ("sbuf", [P, H], "float32"),
+    "hr": ("sbuf", [P, H], "float32"),
+    "ys": ("sbuf", [P, W], "float32"),
+    "acc": ("psum", [P, W], "float32"),
+}
+SEMAPHORES = ["xl", "wl", "sent", "al", "ar", "mm", "cp", "st"]
+
+
+def _pick(allowed, n, avoid):
+    bits = [b for b in range(allowed.bit_length()) if (allowed >> b) & 1 and not (avoid >> b) & 1]
+    m = 0
+    for b in bits[::len(bits) // n][:n]:
+        m |= 1 << b
+    return m
+
+
+def rank_program(g, core, T, topo):
+    r = T.rank_of(core)
+    if r is None:
+        return
+    s = T.sem
+    n = len(T.cores)
+    left, right = T.cores[(r - 1) % n], T.cores[(r + 1) % n]
+
+    def near(a, b):
+        return topo.chip(a) == topo.chip(b)
+
+    def engines(a, b):
+        return K_NEAR if near(a, b) else K_FAR
+
+    g.sync.dma_start(T.xs[:, :], T.x[:, :]).then_inc(s.xl, 16)
+    g.sync.dma_start(T.ws[:, :], T.w[:, :]).then_inc(s.wl, 16)
+
+    sends = [(left, T.xs[:, 0:H], T.hr[:, :], s.ar), (right, T.xs[:, W - H:W], T.hl[:, :], s.al)]
+    sends.sort(key=lambda t: near(core, t[0]))
+    narrow = 0
+    for d, _, _, _ in sends:
+        assert topo.may_write(core, d)
+        if not near(core, d):
+            narrow |= topo.mask(core, d)
+    taken = 0
+    transfers = []
+    for d, src, dst, sem in sends:
+        k = engines(core, d)
+        allowed = topo.mask(core, d)
+        avoid = narrow if near(core, d) else taken
+        m = _pick(allowed, k, avoid | taken)
+        taken |= m
+        rid, pid, _ = topo.addr(d)
+        transfers.append(RemoteDMATransfer(dst_ids=[DstId(rid=rid, pnc=pid)], dma_engine_mask=m, remote_sem=sem,
+                                           src=src, dst=dst))
+    g.wait_ge(s.xl, 16)
+    g.remote_dma_fused(transfers, local_sem=s.sent)
+
+    te = g.tensor
+    w0, w1, w2 = T.ws[:, 0:P], T.ws[:, P:2 * P], T.ws[:, 2 * P:3 * P]
+    te.wait_ge(s.xl, 16)
+    te.wait_ge(s.wl, 16)
+    te.matmul(T.acc[:, 0:W], w1, T.xs[:, 0:W], start=True, stop=False).then_inc(s.mm, 1)
+    te.matmul(T.acc[:, H:W], w0, T.xs[:, 0:W - H], start=False, stop=False).then_inc(s.mm, 1)
+    te.matmul(T.acc[:, 0:W - H], w2, T.xs[:, H:W], start=False, stop=False).then_inc(s.mm, 1)
+    edges = [(left, s.al, T.acc[:, 0:H], w0, T.hl[:, :]), (right, s.ar, T.acc[:, W - H:W], w2, T.hr[:, :])]
+    edges.sort(key=lambda t: not near(t[0], core))
+    for i, (src_core, sem, out, wt, halo) in enumerate(edges):
+        te.wait_ge(sem, engines(src_core, core))
+        te.matmul(out, wt, halo, start=False, stop=(i == len(edges) - 1)).then_inc(s.mm, 1)
+
+    g.vector.wait_ge(s.mm, 5)
+    g.vector.tensor_copy(T.ys[:, :], T.acc[:, :]).then_inc(s.cp, 1)
+    g.sync.wait_ge(s.cp, 1)
+    g.sync.dma_start(T.y[:, :], T.ys[:, :]).then_inc(s.st, 16)
+    g.sync.wait_ge(s.st, 16)
+    g.wait_ge(s.sent, sum(engines(core, d) for d, _, _, _ in sends))

@@ -1,8 +1,10 @@
 from concourse.bass import DstId, RemoteDMATransfer
+from concourse.mybir import AluOpType
 
 P = 128
 W = 128
 H = 8
+BANK = 512
 K_FAR = 4
 K_NEAR = 4
 
@@ -12,9 +14,14 @@ SCRATCH = {
     "hl": ("sbuf", [P, H], "float32"),
     "hr": ("sbuf", [P, H], "float32"),
     "ys": ("sbuf", [P, W], "float32"),
-    "acc": ("psum", [P, W], "float32"),
+    "yl": ("sbuf", [P, H], "float32"),
+    "yr": ("sbuf", [P, H], "float32"),
+    "acc": ("psum", [P, BANK], "float32"),
+    "el": ("psum", [P, BANK], "float32"),
+    "er": ("psum", [P, BANK], "float32"),
 }
-SEMAPHORES = ["xl", "wl", "sent", "al", "ar", "mm", "cp", "st"]
+SEMAPHORES = ["xa", "xb", "xm", "w0l", "w1l", "w2l", "sent", "al", "ar", "mm", "ml", "mr", "ci", "cl", "cr",
+              "si", "sl", "sr"]
 
 
 def _pick(allowed, n, avoid):
@@ -39,46 +46,62 @@ def rank_program(g, core, T, topo):
     def engines(a, b):
         return K_NEAR if near(a, b) else K_FAR
 
-    g.sync.dma_start(T.xs[:, :], T.x[:, :]).then_inc(s.xl, 16)
-    g.sync.dma_start(T.ws[:, :], T.w[:, :]).then_inc(s.wl, 16)
-
-    sends = [(left, T.xs[:, 0:H], T.hr[:, :], s.ar), (right, T.xs[:, W - H:W], T.hl[:, :], s.al)]
+    sends = [(left, (0, H), T.hr[:, :], s.ar, s.xa), (right, (W - H, W), T.hl[:, :], s.al, s.xb)]
     sends.sort(key=lambda t: near(core, t[0]))
+
+    for q, (_, (c0, c1), _, _, ld) in zip([g.sync, g.scalar], sends):
+        q.dma_start(T.xs[:, c0:c1], T.x[:, c0:c1]).then_inc(ld, 16)
+    g.sync.dma_start(T.xs[:, H:W - H], T.x[:, H:W - H]).then_inc(s.xm, 16)
+    g.scalar.dma_start(T.ws[:, P:2 * P], T.w[:, P:2 * P]).then_inc(s.w1l, 16)
+    g.sync.dma_start(T.ws[:, 0:P], T.w[:, 0:P]).then_inc(s.w0l, 16)
+    g.scalar.dma_start(T.ws[:, 2 * P:3 * P], T.w[:, 2 * P:3 * P]).then_inc(s.w2l, 16)
+
     narrow = 0
-    for d, _, _, _ in sends:
-        assert topo.may_write(core, d)
-        if not near(core, d):
-            narrow |= topo.mask(core, d)
+    for t in sends:
+        assert topo.may_write(core, t[0])
+        if not near(core, t[0]):
+            narrow |= topo.mask(core, t[0])
     taken = 0
     transfers = []
-    for d, src, dst, sem in sends:
-        k = engines(core, d)
-        allowed = topo.mask(core, d)
+    for d, (c0, c1), dst, sem, ld in sends:
         avoid = narrow if near(core, d) else taken
-        m = _pick(allowed, k, avoid | taken)
+        m = _pick(topo.mask(core, d), engines(core, d), avoid | taken)
         taken |= m
         rid, pid, _ = topo.addr(d)
         transfers.append(RemoteDMATransfer(dst_ids=[DstId(rid=rid, pnc=pid)], dma_engine_mask=m, remote_sem=sem,
-                                           src=src, dst=dst))
-    g.wait_ge(s.xl, 16)
+                                           src=T.xs[:, c0:c1], dst=dst))
+        g.wait_ge(ld, 16)
     g.remote_dma_fused(transfers, local_sem=s.sent)
 
-    te = g.tensor
+    te, ve = g.tensor, g.vector
     w0, w1, w2 = T.ws[:, 0:P], T.ws[:, P:2 * P], T.ws[:, 2 * P:3 * P]
-    te.wait_ge(s.xl, 16)
-    te.wait_ge(s.wl, 16)
+    te.wait_ge(s.xa, 16)
+    te.wait_ge(s.xb, 16)
+    te.wait_ge(s.xm, 16)
+    te.wait_ge(s.w1l, 16)
     te.matmul(T.acc[:, 0:W], w1, T.xs[:, 0:W], start=True, stop=False).then_inc(s.mm, 1)
+    te.wait_ge(s.w0l, 16)
     te.matmul(T.acc[:, H:W], w0, T.xs[:, 0:W - H], start=False, stop=False).then_inc(s.mm, 1)
-    te.matmul(T.acc[:, 0:W - H], w2, T.xs[:, H:W], start=False, stop=False).then_inc(s.mm, 1)
-    edges = [(left, s.al, T.acc[:, 0:H], w0, T.hl[:, :]), (right, s.ar, T.acc[:, W - H:W], w2, T.hr[:, :])]
-    edges.sort(key=lambda t: not near(t[0], core))
-    for i, (src_core, sem, out, wt, halo) in enumerate(edges):
-        te.wait_ge(sem, engines(src_core, core))
-        te.matmul(out, wt, halo, start=False, stop=(i == len(edges) - 1)).then_inc(s.mm, 1)
+    te.wait_ge(s.w2l, 16)
+    te.matmul(T.acc[:, 0:W - H], w2, T.xs[:, H:W], start=False, stop=True).then_inc(s.mm, 1)
+    ve.wait_ge(s.mm, 3)
+    ve.tensor_copy(T.ys[:, :], T.acc[:, 0:W]).then_inc(s.ci, 1)
+    g.sync.wait_ge(s.ci, 1)
+    g.sync.dma_start(T.y[:, H:W - H], T.ys[:, H:W - H]).then_inc(s.si, 16)
+    ve.wait_ge(s.ci, 1)
 
-    g.vector.wait_ge(s.mm, 5)
-    g.vector.tensor_copy(T.ys[:, :], T.acc[:, :]).then_inc(s.cp, 1)
-    g.sync.wait_ge(s.cp, 1)
-    g.sync.dma_start(T.y[:, :], T.ys[:, :]).then_inc(s.st, 16)
-    g.sync.wait_ge(s.st, 16)
-    g.wait_ge(s.sent, sum(engines(core, d) for d, _, _, _ in sends))
+    edges = [(left, s.al, w0, T.hl, T.el, s.ml, T.ys[:, 0:H], T.yl, s.cl, T.y[:, 0:H], s.sl),
+             (right, s.ar, w2, T.hr, T.er, s.mr, T.ys[:, W - H:W], T.yr, s.cr, T.y[:, W - H:W], s.sr)]
+    edges.sort(key=lambda t: not near(t[0], core))
+    queues = [g.scalar, g.sync]
+    for q, (src_core, arr, wt, halo, ps, md, part, res, cd, ycols, sd) in zip(queues, edges):
+        te.wait_ge(arr, engines(src_core, core))
+        te.matmul(ps[:, 0:H], wt, halo[:, :], start=True, stop=True).then_inc(md, 1)
+        ve.wait_ge(md, 1)
+        ve.tensor_tensor(res[:, :], part, ps[:, 0:H], AluOpType.add).then_inc(cd, 1)
+        q.wait_ge(cd, 1)
+        q.dma_start(ycols, res[:, :]).then_inc(sd, 16)
+    for q, e in zip(queues, edges):
+        q.wait_ge(e[-1], 16)
+    g.sync.wait_ge(s.si, 16)
+    g.wait_ge(s.sent, sum(engines(core, t[0]) for t in sends))

from concourse.bass import DstId, RemoteDMATransfer
from concourse.mybir import AluOpType

P = 128
W = 128
H = 8
BANK = 512
K_FAR = 4
K_NEAR = 4

SCRATCH = {
    "xs": ("sbuf", [P, W], "float32"),
    "ws": ("sbuf", [P, 3 * P], "float32"),
    "hl": ("sbuf", [P, H], "float32"),
    "hr": ("sbuf", [P, H], "float32"),
    "ys": ("sbuf", [P, W], "float32"),
    "yl": ("sbuf", [P, H], "float32"),
    "yr": ("sbuf", [P, H], "float32"),
    "acc": ("psum", [P, BANK], "float32"),
    "el": ("psum", [P, BANK], "float32"),
    "er": ("psum", [P, BANK], "float32"),
}
SEMAPHORES = ["xa", "xb", "xm", "w0l", "w1l", "w2l", "sent", "al", "ar", "mm", "ml", "mr", "ci", "cl", "cr",
              "si", "sl", "sr"]


def _pick(allowed, n, avoid):
    bits = [b for b in range(allowed.bit_length()) if (allowed >> b) & 1 and not (avoid >> b) & 1]
    m = 0
    for b in bits[::len(bits) // n][:n]:
        m |= 1 << b
    return m


def rank_program(g, core, T, topo):
    r = T.rank_of(core)
    if r is None:
        return
    s = T.sem
    n = len(T.cores)
    left, right = T.cores[(r - 1) % n], T.cores[(r + 1) % n]

    def near(a, b):
        return topo.chip(a) == topo.chip(b)

    def engines(a, b):
        return K_NEAR if near(a, b) else K_FAR

    sends = [(left, (0, H), T.hr[:, :], s.ar, s.xa), (right, (W - H, W), T.hl[:, :], s.al, s.xb)]
    sends.sort(key=lambda t: near(core, t[0]))

    for q, (_, (c0, c1), _, _, ld) in zip([g.sync, g.scalar], sends):
        q.dma_start(T.xs[:, c0:c1], T.x[:, c0:c1]).then_inc(ld, 16)
    g.sync.dma_start(T.xs[:, H:W - H], T.x[:, H:W - H]).then_inc(s.xm, 16)
    g.scalar.dma_start(T.ws[:, P:2 * P], T.w[:, P:2 * P]).then_inc(s.w1l, 16)
    g.sync.dma_start(T.ws[:, 0:P], T.w[:, 0:P]).then_inc(s.w0l, 16)
    g.scalar.dma_start(T.ws[:, 2 * P:3 * P], T.w[:, 2 * P:3 * P]).then_inc(s.w2l, 16)

    narrow = 0
    for t in sends:
        assert topo.may_write(core, t[0])
        if not near(core, t[0]):
            narrow |= topo.mask(core, t[0])
    taken = 0
    transfers = []
    for d, (c0, c1), dst, sem, ld in sends:
        avoid = narrow if near(core, d) else taken
        m = _pick(topo.mask(core, d), engines(core, d), avoid | taken)
        taken |= m
        rid, pid, _ = topo.addr(d)
        transfers.append(RemoteDMATransfer(dst_ids=[DstId(rid=rid, pnc=pid)], dma_engine_mask=m, remote_sem=sem,
                                           src=T.xs[:, c0:c1], dst=dst))
        g.wait_ge(ld, 16)
    g.remote_dma_fused(transfers, local_sem=s.sent)

    te, ve = g.tensor, g.vector
    w0, w1, w2 = T.ws[:, 0:P], T.ws[:, P:2 * P], T.ws[:, 2 * P:3 * P]
    te.wait_ge(s.xa, 16)
    te.wait_ge(s.xb, 16)
    te.wait_ge(s.xm, 16)
    te.wait_ge(s.w1l, 16)
    te.matmul(T.acc[:, 0:W], w1, T.xs[:, 0:W], start=True, stop=False).then_inc(s.mm, 1)
    te.wait_ge(s.w0l, 16)
    te.matmul(T.acc[:, H:W], w0, T.xs[:, 0:W - H], start=False, stop=False).then_inc(s.mm, 1)
    te.wait_ge(s.w2l, 16)
    te.matmul(T.acc[:, 0:W - H], w2, T.xs[:, H:W], start=False, stop=True).then_inc(s.mm, 1)
    ve.wait_ge(s.mm, 3)
    ve.tensor_copy(T.ys[:, :], T.acc[:, 0:W]).then_inc(s.ci, 1)
    g.sync.wait_ge(s.ci, 1)
    g.sync.dma_start(T.y[:, H:W - H], T.ys[:, H:W - H]).then_inc(s.si, 16)
    ve.wait_ge(s.ci, 1)

    edges = [(left, s.al, w0, T.hl, T.el, s.ml, T.ys[:, 0:H], T.yl, s.cl, T.y[:, 0:H], s.sl),
             (right, s.ar, w2, T.hr, T.er, s.mr, T.ys[:, W - H:W], T.yr, s.cr, T.y[:, W - H:W], s.sr)]
    edges.sort(key=lambda t: not near(t[0], core))
    queues = [g.scalar, g.sync]
    for q, (src_core, arr, wt, halo, ps, md, part, res, cd, ycols, sd) in zip(queues, edges):
        te.wait_ge(arr, engines(src_core, core))
        te.matmul(ps[:, 0:H], wt, halo[:, :], start=True, stop=True).then_inc(md, 1)
        ve.wait_ge(md, 1)
        ve.tensor_tensor(res[:, :], part, ps[:, 0:H], AluOpType.add).then_inc(cd, 1)
        q.wait_ge(cd, 1)
        q.dma_start(ycols, res[:, :]).then_inc(sd, 16)
    for q, e in zip(queues, edges):
        q.wait_ge(e[-1], 16)
    g.sync.wait_ge(s.si, 16)
    g.wait_ge(s.sent, sum(engines(core, t[0]) for t in sends))
